import numpy as np
import ml_dtypes


def mxq(x, axis, fmt="e4m3"):
    dtype, down = {"e4m3": (ml_dtypes.float8_e4m3fn, 7), "e5m2": (ml_dtypes.float8_e5m2, 14)}[fmt]
    v = np.moveaxis(np.asarray(x, np.float32).astype(ml_dtypes.bfloat16).astype(np.float64), axis, -1)
    blocks = v.reshape(v.shape[:-1] + (-1, 32))
    amax = np.abs(blocks).max(-1, keepdims=True)
    byte = np.maximum(np.where(amax > 0, np.frexp(amax)[1] - 1 + 127, 0) - down, 1)
    scale = np.exp2(byte - 127.0)
    codes = (blocks / scale).astype(np.float32).astype(dtype).astype(np.float64)
    return np.moveaxis((codes * scale).reshape(v.shape), -1, axis)


WIDE = False


def mx_kscale(k):
    if not WIDE:
        return np.ones(k)
    levels = np.array([10, -10, 5, -5, 0])
    if k % 512:
        return np.exp2(np.random.permutation(np.resize(levels, k // 32))).repeat(32)
    a = np.empty((k // 512, 16))
    for p in range(k // 512):
        a[p, :8] = np.random.permutation(np.resize(levels, 8))
        for g in range(8):
            far = levels[np.abs(levels - a[p, g]) >= 10]
            a[p, g + 8] = far[np.random.randint(len(far))]
    return np.exp2(a.ravel()).repeat(32)


def f64(x):
    return np.asarray(x).astype(np.float64)


def striped(idx):
    return np.tile(idx.reshape(-1, 16).T, (8, 1)).astype(np.uint16)


def unstriped(offs):
    return offs[:16].T.reshape(-1).astype(np.int64)


def striped8(idx):
    return np.concatenate([x.reshape(-1, 16).T for x in idx]).astype(np.uint16)


def runs(offs, k):
    lists = np.stack([offs[16 * r : 16 * r + 16].T.reshape(-1) for r in range(8)]).astype(np.int64)
    return lists[np.arange(k) % 512 // 64]


def pack_weight(w):
    k, n = w.shape
    w = f64(np.asarray(w, np.float32).astype(ml_dtypes.bfloat16)).reshape(k // 32, 32, n)
    amax = np.abs(w).max(1)
    byte = np.clip(np.where(amax > 0, np.frexp(amax)[1] - 1 + 127 - 7, 1), 1, 254)
    scaled = (w * np.exp2(127.0 - byte)[:, None, :]).reshape(k, n).astype(np.float32)
    words = np.ascontiguousarray(scaled.reshape(k // 512, 128, 4, n).transpose(0, 1, 3, 2)).astype(ml_dtypes.float8_e4m3fn).view(np.uint8)
    return words, np.ascontiguousarray(byte.astype(np.uint8).reshape(k // 512, 16, n))


def unpack_weight(words, scales):
    g, p, n, _ = words.shape
    vals = np.ascontiguousarray(words).view(ml_dtypes.float8_e4m3fn).astype(np.float64) * np.repeat(np.exp2(scales.astype(np.float64) - 127.0), 8, axis=1)[..., None]
    return vals.transpose(0, 1, 3, 2).reshape(g * 512, n)


def relu(v):
    return np.maximum(v, 0.0)

def planes(y):
    n, m = y.shape
    v = y.astype(np.float32).astype(ml_dtypes.bfloat16).astype(np.float64).reshape(n // 32, 32, m)
    top = np.abs(v).max(1)
    byte = np.clip(np.where(top > 0, np.frexp(top)[1] - 1 + 127 - 7, 1), 1, 254)
    codes = (v * np.exp2(127.0 - byte)[:, None, :]).reshape(n, m).astype(np.float32).astype(ml_dtypes.float8_e4m3fn).view(np.uint8)
    words = codes.reshape(n // 512, 128, 4, m).transpose(0, 1, 3, 2)
    return np.ascontiguousarray(words), np.ascontiguousarray(byte.astype(np.uint8).reshape(n // 512, 16, m))


K, T, S, V, N, H = 512, 2048, 512, 256, 512, 512


def setup_inputs():
    n = np.random.standard_normal
    s = mx_kscale(K)[:, None]
    u = mx_kscale(H)
    packed_xT = pack_weight(n((K, T)) * s)
    packed_w3 = pack_weight(n((H, N)) / np.sqrt(H) / u[:, None])
    perm = np.stack([np.random.permutation(S) for _ in range(8)])
    return {
        "x_words": packed_xT[0],
        "x_scales": packed_xT[1],
        "w1": (n((K, H)) / np.sqrt(K) / s * u).astype(np.float32),
        "w2": (n((H, H)) / np.sqrt(H) / u[:, None] * u).astype(np.float32),
        "w3_words": packed_w3[0],
        "w3_scales": packed_w3[1],
        "offs": striped(np.random.permutation(T)[:S]),
        "la": striped8(perm[:, :V]),
        "lb": striped8(perm[:, V:]),
    }


def reference(x_words, x_scales, w1, w2, w3_words, w3_scales, offs, la, lb):
    xq = unpack_weight(x_words, x_scales)[:, unstriped(offs)]
    y = mxq(f64(w1), 0, "e4m3").T @ xq
    z = y[np.arange(H)[:, None], runs(la, H)]
    h = relu(mxq(f64(w2), 0, "e4m3").T @ mxq(z, 0, "e4m3"))
    o = y[np.arange(H)[:, None], runs(lb, H)] - (0.5 * h)
    p = np.zeros((H, S))
    p[np.arange(H)[:, None], runs(la, H)] = h
    z2 = p.copy()
    z2[np.arange(H)[:, None], runs(lb, H)] = o
    out_0 = unpack_weight(w3_words, w3_scales).T @ mxq(z2, 0, "e4m3")
    return (out_0,) + planes(out_0)

@@ -1,0 +1,185 @@
+from contextlib import ExitStack
+
+import concourse.mybir as mybir
+
+K, T, S, V, N, H = 512, 2048, 512, 256, 512, 512
+FLOPS = 2 * K * H * S + 2 * H * H * V + 2 * H * N * S
+
+F32 = mybir.dt.float32
+BF16 = mybir.dt.bfloat16
+I32 = mybir.dt.int32
+U32 = mybir.dt.uint32
+U16 = mybir.dt.uint16
+U8 = mybir.dt.uint8
+FP8X4 = mybir.dt.float8_e4m3fn_x4
+COPY = mybir.ActivationFunctionType.Copy
+RELU = mybir.ActivationFunctionType.Relu
+ADD = mybir.AluOpType.add
+
+P = 128
+PACK = 4
+HALF = 256
+CHUNK = 128
+
+
+def tile_picked_prunefill_relu_po_kernel(tc, x_words, x_scales, w1, w2, w3_words, w3_scales, offs, la, lb, out_0, out_1, out_2):
+    nc = tc.nc
+    with ExitStack() as ctx:
+        lists = ctx.enter_context(tc.tile_pool(name="lists", bufs=1))
+        sb = ctx.enter_context(tc.tile_pool(name="sb", bufs=1))
+        psum = ctx.enter_context(tc.psum_pool(name="psum", bufs=1))
+
+        def tile(shape, dtype, name, tag=None):
+            return sb.tile(shape, dtype, name=name, tag=tag or name, align_bytes=64)
+
+        def bank(b, name):
+            return psum.tile([P, 512], F32, name=name, tag="bank%d" % b)
+
+        def load_scale_rows(queue, plane, rows):
+            for q in range(4):
+                queue.dma_start(out=plane[32 * q : 32 * q + 4, :].bitcast(I32), in_=rows[4 * q : 4 * q + 4, :].bitcast(I32))
+
+        def load_weight_half(w, half, name, tag=None):
+            raw = tile([P, PACK, HALF], F32, name, tag)
+            nc.sync.dma_start(out=raw[:], in_=w[:, half * HALF : (half + 1) * HALF].rearrange("(p j) c -> p j c", j=PACK))
+            return raw
+
+        def dealt_views(grouped, raw, half):
+            dst = grouped[:].rearrange("p (t m j) -> p m j t", t=PACK, j=PACK)[:, 64 * half : 64 * (half + 1)]
+            src = raw[:].rearrange("p j (m t) -> p m j t", t=PACK)
+            return dst, src
+
+        def quantize(grouped, codes, scales):
+            nc.vector.quantize_mx(out=codes.bitcast(FP8X4), scales=scales, in_=grouped)
+
+        def product(out, w_codes, w_scales, t, codes, scales):
+            cols = slice(P * t, P * (t + 1))
+            nc.tensor.matmul_mx(out=out, lhsT=w_codes[:, cols].bitcast(FP8X4), lhsT_scale=w_scales[:, cols],
+                                rhs=codes.bitcast(FP8X4), rhs_scale=scales, start=True, stop=True)
+
+        offs_sb = lists.tile([P, S // 16], U16, name="offs_sb")
+        la_sb = lists.tile([P, V // 16], U16, name="la_sb")
+        lb_sb = lists.tile([P, V // 16], U16, name="lb_sb")
+
+        x_plane = tile([P, T], U8, "x_plane")
+        w3_plane = tile([P, N], U8, "w3_plane")
+        nc.vector.memset(x_plane[:].bitcast(I32), 0)
+        nc.gpsimd.memset(w3_plane[:].bitcast(I32), 0)
+
+        nc.sync.dma_start(offs_sb[:], offs)
+        nc.sync.dma_start(la_sb[:], la)
+        w1_raw = [load_weight_half(w1, half, "w1_raw%d" % half) for half in range(2)]
+        x_table = tile([P, T], I32, "x_table")
+        nc.sync.dma_start(out=x_table[:], in_=x_words[0].rearrange("p n t -> p (n t)").bitcast(I32))
+        nc.sync.dma_start(lb_sb[:], lb)
+        load_scale_rows(nc.scalar, x_plane, x_scales[0])
+        load_scale_rows(nc.gpsimd, w3_plane, w3_scales[0])
+
+        w1_grouped = tile([P, PACK * H], BF16, "w1_grouped")
+        dst, src = dealt_views(w1_grouped, w1_raw[0], 0)
+        nc.scalar.activation(out=dst, in_=src, func=COPY)
+        dst, src = dealt_views(w1_grouped, w1_raw[1], 1)
+        nc.vector.tensor_copy(out=dst, in_=src)
+        w1_codes = tile([P, H], U32, "w1_codes")
+        w1_scales = tile([P, H], U8, "w1_scales")
+        quantize(w1_grouped[:], w1_codes[:], w1_scales[:])
+
+        w3_table = tile([P, N], I32, "w3_table", "w1_raw0")
+        nc.sync.dma_start(out=w3_table[:], in_=w3_words[0].rearrange("p n t -> p (n t)").bitcast(I32))
+        w2_raw = [load_weight_half(w2, half, "w2_raw%d" % half, tag) for half, tag in enumerate(("w1_raw1", "w1_grouped"))]
+
+        xg_scales = tile([P, S], U8, "xg_scales")
+        nc.vector.tensor_copy(out=xg_scales[:], in_=x_plane[:].indirect(offs_sb[:]))
+        xg_codes = tile([P, S], U32, "xg_codes")
+        halves = [slice(0, HALF), slice(HALF, S)]
+        for half, cols in enumerate(halves):
+            nc.vector.tensor_copy(out=xg_codes[:, cols], in_=x_table[:].bitcast(U32).indirect(offs_sb[:, 16 * half : 16 * (half + 1)]))
+
+        y = [tile([P, S], F32, "y%d" % t) for t in range(PACK)]
+        steps = [(0, halves[0]), (1, halves[0]), (0, halves[1]), (1, halves[1]), (2, slice(0, S)), (3, slice(0, S))]
+        for b, (t, cols) in enumerate(steps):
+            acc = bank(b, "y_acc%d" % b)
+            width = cols.stop - cols.start
+            product(acc[:, :width], w1_codes, w1_scales, t, xg_codes[:, cols], xg_scales[:, cols])
+            nc.scalar.activation(out=y[t][:, cols], in_=acc[:, :width], func=COPY)
+
+        w3_codes = tile([P, N], I32, "w3_codes", "x_plane")
+        w3_sc = tile([P, N], U8, "w3_sc", "x_table")
+        nc.vector.tensor_copy(out=w3_codes[:].rearrange("p (t m) -> p m t", t=PACK), in_=w3_table[:].rearrange("p (m t) -> p m t", t=PACK))
+        nc.vector.tensor_copy(out=w3_sc[:].rearrange("p (t m) -> p m t", t=PACK), in_=w3_plane[:].rearrange("p (m t) -> p m t", t=PACK))
+
+        z_rows = tile([P, PACK, V], BF16, "z_rows")
+        for t in range(PACK):
+            nc.vector.tensor_copy(out=z_rows[:, t, :], in_=y[t][:].indirect(la_sb[:]))
+        z_grouped = tile([P, PACK * V], BF16, "z_grouped")
+        nc.vector.tensor_copy(out=z_grouped[:].rearrange("p (c i t) -> p c t i", i=4, t=PACK), in_=z_rows[:].rearrange("p t (c i) -> p c t i", i=4))
+        y_lb_first = tile([P, 2, V], F32, "y_lb_first", "z_rows")
+        y_lb = [y_lb_first[:, t, :] for t in range(2)]
+        nc.vector.tensor_copy(out=y_lb[0], in_=y[0][:].indirect(lb_sb[:]))
+        z_codes = tile([P, V], U32, "z_codes")
+        z_scales = tile([P, V], U8, "z_scales")
+        quantize(z_grouped[:], z_codes[:], z_scales[:])
+
+        w2_grouped = tile([P, PACK * H], BF16, "w2_grouped", "xg_codes")
+        for half in range(2):
+            dst, src = dealt_views(w2_grouped, w2_raw[half], half)
+            nc.scalar.activation(out=dst, in_=src, func=COPY)
+        w2_codes = tile([P, H], U32, "w2_codes")
+        w2_scales = tile([P, H], U8, "w2_scales")
+        nc.vector.tensor_copy(out=y_lb[1], in_=y[1][:].indirect(lb_sb[:]))
+        quantize(w2_grouped[:], w2_codes[:], w2_scales[:])
+        y_lb_last = tile([P, 2, V], F32, "y_lb_last", "xg_codes")
+        y_lb = y_lb + [y_lb_last[:, t, :] for t in range(2)]
+        for t in range(2, PACK):
+            nc.vector.tensor_copy(out=y_lb[t], in_=y[t][:].indirect(lb_sb[:]))
+
+        order = (2, 0, 1, 3)
+        h = [tile([P, V], F32, "h%d" % t) for t in range(PACK)]
+        loss = [tile([P, V], F32, "loss%d" % t) for t in range(PACK - 1)]
+        for t in order:
+            acc = bank(t, "h_acc%d" % t)
+            product(acc[:, :V], w2_codes, w2_scales, t, z_codes[:], z_scales[:])
+            nc.scalar.activation(out=h[t][:], in_=acc[:, :V], func=RELU)
+            if t != 3:
+                nc.scalar.activation(out=loss[t][:], in_=h[t][:], func=COPY, scale=-0.5)
+
+        z2 = [tile([P, S], F32, "z2_%d" % t) for t in range(PACK)]
+        z2_grouped = tile([P, S, PACK], BF16, "z2_grouped")
+        for t in order:
+            nc.vector.tensor_copy(out=z2[t][:].indirect(la_sb[:]), in_=h[t][:])
+            nc.vector.tensor_tensor(out=z2[t][:].indirect(lb_sb[:]), in0=y_lb[t], in1=loss[t][:], op=ADD)
+            if t != 3:
+                nc.scalar.activation(out=z2_grouped[:, :, t], in_=z2[t][:], func=COPY)
+            if t == 2:
+                loss.append(tile([P, V], F32, "loss3", "z2_2"))
+                nc.scalar.activation(out=loss[3][:], in_=h[3][:], func=COPY, scale=-0.5)
+        z2_codes = tile([P, S], U32, "z2_codes")
+        z2_scales = tile([P, S], U8, "z2_scales")
+        out_codes = tile([P, S], U32, "out_codes")
+        out_scales = tile([P, S], U8, "out_scales")
+        out_rows = out_0.rearrange("(p t) j -> p t j", t=PACK)
+        words_rows = out_1[0].rearrange("p n t -> p (n t)").bitcast(I32)
+        chunks = [slice(c, c + CHUNK) for c in range(0, S, CHUNK)]
+        for c, cols in enumerate(chunks):
+            if c % 2 == 0:
+                nc.vector.tensor_copy(out=z2_grouped[:, cols, PACK - 1], in_=z2[PACK - 1][:, cols])
+            else:
+                nc.scalar.activation(out=z2_grouped[:, cols, PACK - 1], in_=z2[PACK - 1][:, cols], func=COPY)
+        for cols in chunks:
+            quantize(z2_grouped[:, cols, :].rearrange("p c t -> p (c t)"), z2_codes[:, cols], z2_scales[:, cols])
+        for c, cols in enumerate(chunks):
+            acc = bank(4 + c, "out_acc%d" % c)
+            for t in range(PACK):
+                product(acc[:, CHUNK * t : CHUNK * (t + 1)], w3_codes, w3_sc, t, z2_codes[:, cols], z2_scales[:, cols])
+            staged = tile([P, PACK, CHUNK], F32, "staged%d" % c)
+            nc.scalar.activation(out=staged[:].rearrange("p t c -> p (t c)"), in_=acc[:], func=COPY)
+            nc.sync.dma_start(out=out_rows[:, :, cols], in_=staged[:])
+            grouped = tile([P, PACK * CHUNK], BF16, "out_grouped%d" % c)
+            nc.vector.tensor_copy(out=grouped[:].rearrange("p (c i t) -> p c t i", i=4, t=PACK), in_=staged[:].rearrange("p t (c i) -> p c t i", i=4))
+            quantize(grouped[:], out_codes[:, cols], out_scales[:, cols])
+            if c % 2 == 1:
+                both = slice(cols.start - CHUNK, cols.stop)
+                nc.sync.dma_start(out=words_rows[:, both], in_=out_codes[:, both].bitcast(I32))
+        for q in range(4):
+            queue = nc.sync if q % 2 == 0 else nc.scalar
+            queue.dma_start(out=out_2[0, 4 * q : 4 * q + 4, :].bitcast(I32), in_=out_scales[32 * q : 32 * q + 4, :].bitcast(I32))

@@ -27,6 +27,8 @@ def tile_picked_prunefill_relu_po_kernel(tc, x_words, x_scales, w1, w2, w3_words
     with ExitStack() as ctx:
         lists = ctx.enter_context(tc.tile_pool(name="lists", bufs=1))
         sb = ctx.enter_context(tc.tile_pool(name="sb", bufs=1))
+        table = ctx.enter_context(tc.tile_pool(name="table", bufs=1))
+        staging = ctx.enter_context(tc.tile_pool(name="staging", bufs=1))
         psum = ctx.enter_context(tc.psum_pool(name="psum", bufs=1))
 
         def tile(shape, dtype, name, tag=None):
@@ -39,14 +41,14 @@ def tile_picked_prunefill_relu_po_kernel(tc, x_words, x_scales, w1, w2, w3_words
             for q in range(4):
                 queue.dma_start(out=plane[32 * q : 32 * q + 4, :].bitcast(I32), in_=rows[4 * q : 4 * q + 4, :].bitcast(I32))
 
-        def load_weight_half(w, half, name, tag=None):
-            raw = tile([P, PACK, HALF], F32, name, tag)
-            nc.sync.dma_start(out=raw[:], in_=w[:, half * HALF : (half + 1) * HALF].rearrange("(p j) c -> p j c", j=PACK))
+        def load_weight(w, name, offset):
+            raw = staging.tile([P, PACK, H], F32, name=name, align_bytes=64, offset=offset)
+            nc.sync.dma_start(out=raw[:], in_=w.rearrange("(p j) c -> p j c", j=PACK))
             return raw
 
-        def dealt_views(grouped, raw, half):
-            dst = grouped[:].rearrange("p (t m j) -> p m j t", t=PACK, j=PACK)[:, 64 * half : 64 * (half + 1)]
-            src = raw[:].rearrange("p j (m t) -> p m j t", t=PACK)
+        def dealt_views(grouped, raw, rows):
+            dst = grouped[:].rearrange("p (t m j) -> p m j t", t=PACK, j=PACK)[:, rows]
+            src = raw[:].rearrange("p j (m t) -> p m j t", t=PACK)[:, rows]
             return dst, src
 
         def quantize(grouped, codes, scales):
@@ -68,28 +70,28 @@ def tile_picked_prunefill_relu_po_kernel(tc, x_words, x_scales, w1, w2, w3_words
 
         nc.sync.dma_start(offs_sb[:], offs)
         nc.sync.dma_start(la_sb[:], la)
-        w1_raw = [load_weight_half(w1, half, "w1_raw%d" % half) for half in range(2)]
-        x_table = tile([P, T], I32, "x_table")
+        w1_raw = load_weight(w1, "w1_raw", 0)
+        x_table = table.tile([P, T], I32, name="x_table", align_bytes=64, offset=0)
         nc.sync.dma_start(out=x_table[:], in_=x_words[0].rearrange("p n t -> p (n t)").bitcast(I32))
         nc.sync.dma_start(lb_sb[:], lb)
         load_scale_rows(nc.scalar, x_plane, x_scales[0])
         load_scale_rows(nc.gpsimd, w3_plane, w3_scales[0])
 
         w1_grouped = tile([P, PACK * H], BF16, "w1_grouped")
-        dst, src = dealt_views(w1_grouped, w1_raw[0], 0)
+        dst, src = dealt_views(w1_grouped, w1_raw, slice(0, 44))
         nc.scalar.activation(out=dst, in_=src, func=COPY)
-        dst, src = dealt_views(w1_grouped, w1_raw[1], 1)
+        dst, src = dealt_views(w1_grouped, w1_raw, slice(44, P))
         nc.vector.tensor_copy(out=dst, in_=src)
         w1_codes = tile([P, H], U32, "w1_codes")
         w1_scales = tile([P, H], U8, "w1_scales")
         quantize(w1_grouped[:], w1_codes[:], w1_scales[:])
-
-        w3_table = tile([P, N], I32, "w3_table", "w1_raw0")
-        nc.sync.dma_start(out=w3_table[:], in_=w3_words[0].rearrange("p n t -> p (n t)").bitcast(I32))
-        w2_raw = [load_weight_half(w2, half, "w2_raw%d" % half, tag) for half, tag in enumerate(("w1_raw1", "w1_grouped"))]
-
-        xg_scales = tile([P, S], U8, "xg_scales")
+        xg_scales = tile([P, S], U8, "xg_scales", "w1_grouped")
         nc.vector.tensor_copy(out=xg_scales[:], in_=x_plane[:].indirect(offs_sb[:]))
+
+        w3_table = staging.tile([P, N], I32, name="w3_table", align_bytes=64, offset=0)
+        nc.sync.dma_start(out=w3_table[:], in_=w3_words[0].rearrange("p n t -> p (n t)").bitcast(I32))
+        w2_raw = load_weight(w2, "w2_raw", 4 * N)
+
         xg_codes = tile([P, S], U32, "xg_codes")
         halves = [slice(0, HALF), slice(HALF, S)]
         for half, cols in enumerate(halves):
@@ -103,17 +105,17 @@ def tile_picked_prunefill_relu_po_kernel(tc, x_words, x_scales, w1, w2, w3_words
             product(acc[:, :width], w1_codes, w1_scales, t, xg_codes[:, cols], xg_scales[:, cols])
             nc.scalar.activation(out=y[t][:, cols], in_=acc[:, :width], func=COPY)
 
-        w3_codes = tile([P, N], I32, "w3_codes", "x_plane")
-        w3_sc = tile([P, N], U8, "w3_sc", "x_table")
+        w3_codes = table.tile([P, N], I32, name="w3_codes", align_bytes=64, offset=0)
+        w3_sc = table.tile([P, N], U8, name="w3_sc", align_bytes=64, offset=4 * N)
+        nc.vector.tensor_copy(out=w3_sc[:].rearrange("p (t m) -> p t m", t=PACK), in_=w3_plane[:].rearrange("p (m t) -> p t m", t=PACK))
         nc.vector.tensor_copy(out=w3_codes[:].rearrange("p (t m) -> p m t", t=PACK), in_=w3_table[:].rearrange("p (m t) -> p m t", t=PACK))
-        nc.vector.tensor_copy(out=w3_sc[:].rearrange("p (t m) -> p m t", t=PACK), in_=w3_plane[:].rearrange("p (m t) -> p m t", t=PACK))
 
-        z_rows = tile([P, PACK, V], BF16, "z_rows")
+        z_rows = staging.tile([P, PACK, V], BF16, name="z_rows", align_bytes=64, offset=0)
         for t in range(PACK):
             nc.vector.tensor_copy(out=z_rows[:, t, :], in_=y[t][:].indirect(la_sb[:]))
         z_grouped = tile([P, PACK * V], BF16, "z_grouped")
         nc.vector.tensor_copy(out=z_grouped[:].rearrange("p (c i t) -> p c t i", i=4, t=PACK), in_=z_rows[:].rearrange("p t (c i) -> p c t i", i=4))
-        y_lb_first = tile([P, 2, V], F32, "y_lb_first", "z_rows")
+        y_lb_first = staging.tile([P, 2, V], F32, name="y_lb_first", align_bytes=64, offset=0)
         y_lb = [y_lb_first[:, t, :] for t in range(2)]
         nc.vector.tensor_copy(out=y_lb[0], in_=y[0][:].indirect(lb_sb[:]))
         z_codes = tile([P, V], U32, "z_codes")
@@ -121,9 +123,8 @@ def tile_picked_prunefill_relu_po_kernel(tc, x_words, x_scales, w1, w2, w3_words
         quantize(z_grouped[:], z_codes[:], z_scales[:])
 
         w2_grouped = tile([P, PACK * H], BF16, "w2_grouped", "xg_codes")
-        for half in range(2):
-            dst, src = dealt_views(w2_grouped, w2_raw[half], half)
-            nc.scalar.activation(out=dst, in_=src, func=COPY)
+        dst, src = dealt_views(w2_grouped, w2_raw, slice(0, P))
+        nc.scalar.activation(out=dst, in_=src, func=COPY)
         w2_codes = tile([P, H], U32, "w2_codes")
         w2_scales = tile([P, H], U8, "w2_scales")
         nc.vector.tensor_copy(out=y_lb[1], in_=y[1][:].indirect(lb_sb[:]))
@@ -177,8 +178,8 @@ def tile_picked_prunefill_relu_po_kernel(tc, x_words, x_scales, w1, w2, w3_words
             grouped = tile([P, PACK * CHUNK], BF16, "out_grouped%d" % c)
             nc.vector.tensor_copy(out=grouped[:].rearrange("p (c i t) -> p c t i", i=4, t=PACK), in_=staged[:].rearrange("p t (c i) -> p c t i", i=4))
             quantize(grouped[:], out_codes[:, cols], out_scales[:, cols])
-            if c % 2 == 1:
-                both = slice(cols.start - CHUNK, cols.stop)
+            if c >= 2:
+                both = slice(0 if c == 2 else cols.start, cols.stop)
                 nc.sync.dma_start(out=words_rows[:, both], in_=out_codes[:, both].bitcast(I32))
         for q in range(4):
             queue = nc.sync if q % 2 == 0 else nc.scalar

@@ -92,7 +92,7 @@ def tile_picked_prunefill_relu_po_kernel(tc, x_words, x_scales, w1, w2, w3_words
         nc.sync.dma_start(out=w3_table[:], in_=w3_words[0].rearrange("p n t -> p (n t)").bitcast(I32))
         w2_raw = load_weight(w2, "w2_raw", 4 * N)
 
-        xg_codes = tile([P, S], U32, "xg_codes")
+        xg_codes = tile([P, S], U32, "xg_codes", "x_plane")
         halves = [slice(0, HALF), slice(HALF, S)]
         for half, cols in enumerate(halves):
             nc.vector.tensor_copy(out=xg_codes[:, cols], in_=x_table[:].bitcast(U32).indirect(offs_sb[:, 16 * half : 16 * (half + 1)]))
@@ -122,14 +122,14 @@ def tile_picked_prunefill_relu_po_kernel(tc, x_words, x_scales, w1, w2, w3_words
         z_scales = tile([P, V], U8, "z_scales")
         quantize(z_grouped[:], z_codes[:], z_scales[:])
 
-        w2_grouped = tile([P, PACK * H], BF16, "w2_grouped", "xg_codes")
+        w2_grouped = tile([P, PACK * H], BF16, "w2_grouped", "x_plane")
         dst, src = dealt_views(w2_grouped, w2_raw, slice(0, P))
         nc.scalar.activation(out=dst, in_=src, func=COPY)
         w2_codes = tile([P, H], U32, "w2_codes")
         w2_scales = tile([P, H], U8, "w2_scales")
         nc.vector.tensor_copy(out=y_lb[1], in_=y[1][:].indirect(lb_sb[:]))
         quantize(w2_grouped[:], w2_codes[:], w2_scales[:])
-        y_lb_last = tile([P, 2, V], F32, "y_lb_last", "xg_codes")
+        y_lb_last = tile([P, 2, V], F32, "y_lb_last", "x_plane")
         y_lb = y_lb + [y_lb_last[:, t, :] for t in range(2)]
         for t in range(2, PACK):
             nc.vector.tensor_copy(out=y_lb[t], in_=y[t][:].indirect(lb_sb[:]))

@@ -29,6 +29,7 @@ def tile_picked_prunefill_relu_po_kernel(tc, x_words, x_scales, w1, w2, w3_words
         sb = ctx.enter_context(tc.tile_pool(name="sb", bufs=1))
         table = ctx.enter_context(tc.tile_pool(name="table", bufs=1))
         staging = ctx.enter_context(tc.tile_pool(name="staging", bufs=1))
+        early = ctx.enter_context(tc.tile_pool(name="early", bufs=1))
         psum = ctx.enter_context(tc.psum_pool(name="psum", bufs=1))
 
         def tile(shape, dtype, name, tag=None):
@@ -37,8 +38,8 @@ def tile_picked_prunefill_relu_po_kernel(tc, x_words, x_scales, w1, w2, w3_words
         def bank(b, name):
             return psum.tile([P, 512], F32, name=name, tag="bank%d" % b)
 
-        def load_scale_rows(queue, plane, rows):
-            for q in range(4):
+        def load_scale_rows(queues, plane, rows):
+            for q, queue in enumerate(queues):
                 queue.dma_start(out=plane[32 * q : 32 * q + 4, :].bitcast(I32), in_=rows[4 * q : 4 * q + 4, :].bitcast(I32))
 
         def load_weight(w, name, offset):
@@ -63,36 +64,41 @@ def tile_picked_prunefill_relu_po_kernel(tc, x_words, x_scales, w1, w2, w3_words
         la_sb = lists.tile([P, V // 16], U16, name="la_sb")
         lb_sb = lists.tile([P, V // 16], U16, name="lb_sb")
 
-        x_plane = tile([P, T], U8, "x_plane")
+        x_plane = early.tile([P, T], U8, name="x_plane", align_bytes=64, offset=0)
+        x_rows = tile([P, T], U8, "x_rows")
         w3_plane = tile([P, N], U8, "w3_plane")
         nc.vector.memset(x_plane[:].bitcast(I32), 0)
         nc.gpsimd.memset(w3_plane[:].bitcast(I32), 0)
 
+        load_scale_rows([nc.sync, nc.scalar, nc.sync, nc.scalar], x_rows, x_scales[0])
         nc.sync.dma_start(offs_sb[:], offs)
-        nc.sync.dma_start(la_sb[:], la)
         w1_raw = load_weight(w1, "w1_raw", 0)
         x_table = table.tile([P, T], I32, name="x_table", align_bytes=64, offset=0)
         nc.sync.dma_start(out=x_table[:], in_=x_words[0].rearrange("p n t -> p (n t)").bitcast(I32))
+        nc.sync.dma_start(la_sb[:], la)
         nc.sync.dma_start(lb_sb[:], lb)
-        load_scale_rows(nc.scalar, x_plane, x_scales[0])
-        load_scale_rows(nc.gpsimd, w3_plane, w3_scales[0])
+        load_scale_rows([nc.gpsimd] * 4, w3_plane, w3_scales[0])
 
-        w1_grouped = tile([P, PACK * H], BF16, "w1_grouped")
-        dst, src = dealt_views(w1_grouped, w1_raw, slice(0, 44))
+        for q in range(4):
+            rows = slice(32 * q, 32 * q + 4)
+            nc.vector.tensor_copy(out=x_plane[rows, :].bitcast(I32), in_=x_rows[rows, :].bitcast(I32))
+        xg_scales = tile([P, S], U8, "xg_scales")
+        nc.vector.tensor_copy(out=xg_scales[:], in_=x_plane[:].indirect(offs_sb[:]))
+
+        w1_grouped = early.tile([P, PACK * H], BF16, name="w1_grouped", align_bytes=64, offset=T)
+        dst, src = dealt_views(w1_grouped, w1_raw, slice(0, 64))
         nc.scalar.activation(out=dst, in_=src, func=COPY)
-        dst, src = dealt_views(w1_grouped, w1_raw, slice(44, P))
+        dst, src = dealt_views(w1_grouped, w1_raw, slice(64, P))
         nc.vector.tensor_copy(out=dst, in_=src)
         w1_codes = tile([P, H], U32, "w1_codes")
         w1_scales = tile([P, H], U8, "w1_scales")
         quantize(w1_grouped[:], w1_codes[:], w1_scales[:])
-        xg_scales = tile([P, S], U8, "xg_scales", "w1_grouped")
-        nc.vector.tensor_copy(out=xg_scales[:], in_=x_plane[:].indirect(offs_sb[:]))
 
         w3_table = staging.tile([P, N], I32, name="w3_table", align_bytes=64, offset=0)
         nc.sync.dma_start(out=w3_table[:], in_=w3_words[0].rearrange("p n t -> p (n t)").bitcast(I32))
         w2_raw = load_weight(w2, "w2_raw", 4 * N)
 
-        xg_codes = tile([P, S], U32, "xg_codes", "x_plane")
+        xg_codes = early.tile([P, S], U32, name="xg_codes", align_bytes=64, offset=T // 2)
         halves = [slice(0, HALF), slice(HALF, S)]
         for half, cols in enumerate(halves):
             nc.vector.tensor_copy(out=xg_codes[:, cols], in_=x_table[:].bitcast(U32).indirect(offs_sb[:, 16 * half : 16 * (half + 1)]))
@@ -122,14 +128,14 @@ def tile_picked_prunefill_relu_po_kernel(tc, x_words, x_scales, w1, w2, w3_words
         z_scales = tile([P, V], U8, "z_scales")
         quantize(z_grouped[:], z_codes[:], z_scales[:])
 
-        w2_grouped = tile([P, PACK * H], BF16, "w2_grouped", "x_plane")
+        w2_grouped = early.tile([P, PACK * H], BF16, name="w2_grouped", align_bytes=64, offset=0)
         dst, src = dealt_views(w2_grouped, w2_raw, slice(0, P))
         nc.scalar.activation(out=dst, in_=src, func=COPY)
         w2_codes = tile([P, H], U32, "w2_codes")
         w2_scales = tile([P, H], U8, "w2_scales")
         nc.vector.tensor_copy(out=y_lb[1], in_=y[1][:].indirect(lb_sb[:]))
         quantize(w2_grouped[:], w2_codes[:], w2_scales[:])
-        y_lb_last = tile([P, 2, V], F32, "y_lb_last", "x_plane")
+        y_lb_last = early.tile([P, 2, V], F32, name="y_lb_last", align_bytes=64, offset=0)
         y_lb = y_lb + [y_lb_last[:, t, :] for t in range(2)]
         for t in range(2, PACK):
             nc.vector.tensor_copy(out=y_lb[t], in_=y[t][:].indirect(lb_sb[:]))

@@ -18,8 +18,14 @@ ADD = mybir.AluOpType.add
 
 P = 128
 PACK = 4
-HALF = 256
-CHUNK = 128
+QUADRANTS = 4
+BANK = 512
+HALF = S // 2
+CHUNK = BANK // PACK
+W1_SCALAR = P // 2
+W3_BYTES = 4 * N
+LAST = PACK - 1
+FIRST = LAST - 1
 
 
 def tile_picked_prunefill_relu_po_kernel(tc, x_words, x_scales, w1, w2, w3_words, w3_scales, offs, la, lb, out_0, out_1, out_2):
@@ -35,36 +41,50 @@ def tile_picked_prunefill_relu_po_kernel(tc, x_words, x_scales, w1, w2, w3_words
         def tile(shape, dtype, name, tag=None):
             return sb.tile(shape, dtype, name=name, tag=tag or name, align_bytes=64)
 
+        def placed(pool, offset, shape, dtype, name):
+            return pool.tile(shape, dtype, name=name, align_bytes=64, offset=offset)
+
         def bank(b, name):
-            return psum.tile([P, 512], F32, name=name, tag="bank%d" % b)
+            return psum.tile([P, BANK], F32, name=name, tag="bank%d" % b)
+
+        def live(q):
+            return slice(32 * q, 32 * q + 4)
 
         def load_scale_rows(queues, plane, rows):
             for q, queue in enumerate(queues):
-                queue.dma_start(out=plane[32 * q : 32 * q + 4, :].bitcast(I32), in_=rows[4 * q : 4 * q + 4, :].bitcast(I32))
+                queue.dma_start(out=plane[live(q), :].bitcast(I32), in_=rows[4 * q : 4 * q + 4, :].bitcast(I32))
 
         def load_weight(w, name, offset):
-            raw = staging.tile([P, PACK, H], F32, name=name, align_bytes=64, offset=offset)
+            raw = placed(staging, offset, [P, PACK, H], F32, name)
             nc.sync.dma_start(out=raw[:], in_=w.rearrange("(p j) c -> p j c", j=PACK))
             return raw
 
-        def dealt_views(grouped, raw, rows):
-            dst = grouped[:].rearrange("p (t m j) -> p m j t", t=PACK, j=PACK)[:, rows]
-            src = raw[:].rearrange("p j (m t) -> p m j t", t=PACK)[:, rows]
+        def dealt_views(grouped, raw, ms):
+            dst = grouped[:].rearrange("p (t m j) -> p m j t", t=PACK, j=PACK)[:, ms]
+            src = raw[:].rearrange("p j (m t) -> p m j t", t=PACK)[:, ms]
             return dst, src
+
+        def group(grouped, row_sets):
+            nc.vector.tensor_copy(
+                out=grouped[:].rearrange("p (c i t) -> p c t i", i=4, t=PACK),
+                in_=row_sets[:].rearrange("p t (c i) -> p c t i", i=4),
+            )
 
         def quantize(grouped, codes, scales):
             nc.vector.quantize_mx(out=codes.bitcast(FP8X4), scales=scales, in_=grouped)
 
         def product(out, w_codes, w_scales, t, codes, scales):
             cols = slice(P * t, P * (t + 1))
-            nc.tensor.matmul_mx(out=out, lhsT=w_codes[:, cols].bitcast(FP8X4), lhsT_scale=w_scales[:, cols],
-                                rhs=codes.bitcast(FP8X4), rhs_scale=scales, start=True, stop=True)
+            nc.tensor.matmul_mx(
+                out=out, lhsT=w_codes[:, cols].bitcast(FP8X4), lhsT_scale=w_scales[:, cols],
+                rhs=codes.bitcast(FP8X4), rhs_scale=scales, start=True, stop=True,
+            )
 
         offs_sb = lists.tile([P, S // 16], U16, name="offs_sb")
         la_sb = lists.tile([P, V // 16], U16, name="la_sb")
         lb_sb = lists.tile([P, V // 16], U16, name="lb_sb")
 
-        x_plane = early.tile([P, T], U8, name="x_plane", align_bytes=64, offset=0)
+        x_plane = placed(early, 0, [P, T], U8, "x_plane")
         x_rows = tile([P, T], U8, "x_rows")
         w3_plane = tile([P, N], U8, "w3_plane")
         nc.vector.memset(x_plane[:].bitcast(I32), 0)
@@ -73,81 +93,82 @@ def tile_picked_prunefill_relu_po_kernel(tc, x_words, x_scales, w1, w2, w3_words
         load_scale_rows([nc.sync, nc.scalar, nc.sync, nc.scalar], x_rows, x_scales[0])
         nc.sync.dma_start(offs_sb[:], offs)
         w1_raw = load_weight(w1, "w1_raw", 0)
-        x_table = table.tile([P, T], I32, name="x_table", align_bytes=64, offset=0)
+        x_table = placed(table, 0, [P, T], I32, "x_table")
         nc.sync.dma_start(out=x_table[:], in_=x_words[0].rearrange("p n t -> p (n t)").bitcast(I32))
         nc.sync.dma_start(la_sb[:], la)
         nc.sync.dma_start(lb_sb[:], lb)
-        load_scale_rows([nc.gpsimd] * 4, w3_plane, w3_scales[0])
+        load_scale_rows([nc.gpsimd, nc.sync, nc.gpsimd, nc.sync], w3_plane, w3_scales[0])
 
-        for q in range(4):
-            rows = slice(32 * q, 32 * q + 4)
-            nc.vector.tensor_copy(out=x_plane[rows, :].bitcast(I32), in_=x_rows[rows, :].bitcast(I32))
+        for q in range(QUADRANTS):
+            nc.vector.tensor_copy(out=x_plane[live(q), :].bitcast(I32), in_=x_rows[live(q), :].bitcast(I32))
         xg_scales = tile([P, S], U8, "xg_scales")
         nc.vector.tensor_copy(out=xg_scales[:], in_=x_plane[:].indirect(offs_sb[:]))
 
-        w1_grouped = early.tile([P, PACK * H], BF16, name="w1_grouped", align_bytes=64, offset=T)
-        dst, src = dealt_views(w1_grouped, w1_raw, slice(0, 64))
+        w1_grouped = placed(early, T, [P, PACK * H], BF16, "w1_grouped")
+        dst, src = dealt_views(w1_grouped, w1_raw, slice(0, W1_SCALAR))
         nc.scalar.activation(out=dst, in_=src, func=COPY)
-        dst, src = dealt_views(w1_grouped, w1_raw, slice(64, P))
+        dst, src = dealt_views(w1_grouped, w1_raw, slice(W1_SCALAR, P))
         nc.vector.tensor_copy(out=dst, in_=src)
         w1_codes = tile([P, H], U32, "w1_codes")
         w1_scales = tile([P, H], U8, "w1_scales")
         quantize(w1_grouped[:], w1_codes[:], w1_scales[:])
 
-        w3_table = staging.tile([P, N], I32, name="w3_table", align_bytes=64, offset=0)
+        w3_table = placed(staging, 0, [P, N], I32, "w3_table")
         nc.sync.dma_start(out=w3_table[:], in_=w3_words[0].rearrange("p n t -> p (n t)").bitcast(I32))
-        w2_raw = load_weight(w2, "w2_raw", 4 * N)
+        w2_raw = load_weight(w2, "w2_raw", W3_BYTES)
 
-        xg_codes = early.tile([P, S], U32, name="xg_codes", align_bytes=64, offset=T // 2)
+        xg_codes = placed(early, T // 2, [P, S], U32, "xg_codes")
         halves = [slice(0, HALF), slice(HALF, S)]
-        for half, cols in enumerate(halves):
-            nc.vector.tensor_copy(out=xg_codes[:, cols], in_=x_table[:].bitcast(U32).indirect(offs_sb[:, 16 * half : 16 * (half + 1)]))
+        for cols in halves:
+            entries = offs_sb[:, cols.start // 16 : cols.stop // 16]
+            nc.vector.tensor_copy(out=xg_codes[:, cols], in_=x_table[:].bitcast(U32).indirect(entries))
 
         y = [tile([P, S], F32, "y%d" % t) for t in range(PACK)]
-        steps = [(0, halves[0]), (1, halves[0]), (0, halves[1]), (1, halves[1]), (2, slice(0, S)), (3, slice(0, S))]
+        steps = [(t, cols) for cols in halves for t in range(2)] + [(t, slice(0, S)) for t in range(2, PACK)]
         for b, (t, cols) in enumerate(steps):
             acc = bank(b, "y_acc%d" % b)
             width = cols.stop - cols.start
             product(acc[:, :width], w1_codes, w1_scales, t, xg_codes[:, cols], xg_scales[:, cols])
             nc.scalar.activation(out=y[t][:, cols], in_=acc[:, :width], func=COPY)
 
-        w3_codes = table.tile([P, N], I32, name="w3_codes", align_bytes=64, offset=0)
-        w3_sc = table.tile([P, N], U8, name="w3_sc", align_bytes=64, offset=4 * N)
+        w3_codes = placed(table, 0, [P, N], I32, "w3_codes")
+        w3_sc = placed(table, W3_BYTES, [P, N], U8, "w3_sc")
         nc.vector.tensor_copy(out=w3_sc[:].rearrange("p (t m) -> p t m", t=PACK), in_=w3_plane[:].rearrange("p (m t) -> p t m", t=PACK))
         nc.vector.tensor_copy(out=w3_codes[:].rearrange("p (t m) -> p m t", t=PACK), in_=w3_table[:].rearrange("p (m t) -> p m t", t=PACK))
 
-        z_rows = staging.tile([P, PACK, V], BF16, name="z_rows", align_bytes=64, offset=0)
+        z_rows = placed(staging, 0, [P, PACK, V], BF16, "z_rows")
         for t in range(PACK):
             nc.vector.tensor_copy(out=z_rows[:, t, :], in_=y[t][:].indirect(la_sb[:]))
         z_grouped = tile([P, PACK * V], BF16, "z_grouped")
-        nc.vector.tensor_copy(out=z_grouped[:].rearrange("p (c i t) -> p c t i", i=4, t=PACK), in_=z_rows[:].rearrange("p t (c i) -> p c t i", i=4))
-        y_lb_first = staging.tile([P, 2, V], F32, name="y_lb_first", align_bytes=64, offset=0)
+        group(z_grouped, z_rows)
+
+        y_lb_first = placed(staging, 0, [P, 2, V], F32, "y_lb_first")
         y_lb = [y_lb_first[:, t, :] for t in range(2)]
         nc.vector.tensor_copy(out=y_lb[0], in_=y[0][:].indirect(lb_sb[:]))
         z_codes = tile([P, V], U32, "z_codes")
         z_scales = tile([P, V], U8, "z_scales")
         quantize(z_grouped[:], z_codes[:], z_scales[:])
 
-        w2_grouped = early.tile([P, PACK * H], BF16, name="w2_grouped", align_bytes=64, offset=0)
+        w2_grouped = placed(early, 0, [P, PACK * H], BF16, "w2_grouped")
         dst, src = dealt_views(w2_grouped, w2_raw, slice(0, P))
         nc.scalar.activation(out=dst, in_=src, func=COPY)
         w2_codes = tile([P, H], U32, "w2_codes")
         w2_scales = tile([P, H], U8, "w2_scales")
         nc.vector.tensor_copy(out=y_lb[1], in_=y[1][:].indirect(lb_sb[:]))
         quantize(w2_grouped[:], w2_codes[:], w2_scales[:])
-        y_lb_last = early.tile([P, 2, V], F32, name="y_lb_last", align_bytes=64, offset=0)
+        y_lb_last = placed(early, 0, [P, 2, V], F32, "y_lb_last")
         y_lb = y_lb + [y_lb_last[:, t, :] for t in range(2)]
         for t in range(2, PACK):
             nc.vector.tensor_copy(out=y_lb[t], in_=y[t][:].indirect(lb_sb[:]))
 
-        order = (2, 0, 1, 3)
+        order = [FIRST] + list(range(FIRST)) + [LAST]
         h = [tile([P, V], F32, "h%d" % t) for t in range(PACK)]
-        loss = [tile([P, V], F32, "loss%d" % t) for t in range(PACK - 1)]
+        loss = [tile([P, V], F32, "loss%d" % t) for t in range(LAST)]
         for t in order:
             acc = bank(t, "h_acc%d" % t)
             product(acc[:, :V], w2_codes, w2_scales, t, z_codes[:], z_scales[:])
             nc.scalar.activation(out=h[t][:], in_=acc[:, :V], func=RELU)
-            if t != 3:
+            if t != LAST:
                 nc.scalar.activation(out=loss[t][:], in_=h[t][:], func=COPY, scale=-0.5)
 
         z2 = [tile([P, S], F32, "z2_%d" % t) for t in range(PACK)]
@@ -155,38 +176,40 @@ def tile_picked_prunefill_relu_po_kernel(tc, x_words, x_scales, w1, w2, w3_words
         for t in order:
             nc.vector.tensor_copy(out=z2[t][:].indirect(la_sb[:]), in_=h[t][:])
             nc.vector.tensor_tensor(out=z2[t][:].indirect(lb_sb[:]), in0=y_lb[t], in1=loss[t][:], op=ADD)
-            if t != 3:
+            if t != LAST:
                 nc.scalar.activation(out=z2_grouped[:, :, t], in_=z2[t][:], func=COPY)
-            if t == 2:
-                loss.append(tile([P, V], F32, "loss3", "z2_2"))
-                nc.scalar.activation(out=loss[3][:], in_=h[3][:], func=COPY, scale=-0.5)
+            if t == FIRST:
+                loss.append(tile([P, V], F32, "loss%d" % LAST, "z2_%d" % FIRST))
+                nc.scalar.activation(out=loss[LAST][:], in_=h[LAST][:], func=COPY, scale=-0.5)
+
         z2_codes = tile([P, S], U32, "z2_codes")
         z2_scales = tile([P, S], U8, "z2_scales")
         out_codes = tile([P, S], U32, "out_codes")
         out_scales = tile([P, S], U8, "out_scales")
         out_rows = out_0.rearrange("(p t) j -> p t j", t=PACK)
         words_rows = out_1[0].rearrange("p n t -> p (n t)").bitcast(I32)
-        chunks = [slice(c, c + CHUNK) for c in range(0, S, CHUNK)]
+        chunks = [slice(start, start + CHUNK) for start in range(0, S, CHUNK)]
         for c, cols in enumerate(chunks):
             if c % 2 == 0:
-                nc.vector.tensor_copy(out=z2_grouped[:, cols, PACK - 1], in_=z2[PACK - 1][:, cols])
+                nc.vector.tensor_copy(out=z2_grouped[:, cols, LAST], in_=z2[LAST][:, cols])
             else:
-                nc.scalar.activation(out=z2_grouped[:, cols, PACK - 1], in_=z2[PACK - 1][:, cols], func=COPY)
+                nc.scalar.activation(out=z2_grouped[:, cols, LAST], in_=z2[LAST][:, cols], func=COPY)
         for cols in chunks:
             quantize(z2_grouped[:, cols, :].rearrange("p c t -> p (c t)"), z2_codes[:, cols], z2_scales[:, cols])
+
+        word_stores = {S - CHUNK: slice(0, S - CHUNK), S: chunks[-1]}
         for c, cols in enumerate(chunks):
-            acc = bank(4 + c, "out_acc%d" % c)
+            acc = bank(PACK + c, "out_acc%d" % c)
             for t in range(PACK):
                 product(acc[:, CHUNK * t : CHUNK * (t + 1)], w3_codes, w3_sc, t, z2_codes[:, cols], z2_scales[:, cols])
             staged = tile([P, PACK, CHUNK], F32, "staged%d" % c)
             nc.scalar.activation(out=staged[:].rearrange("p t c -> p (t c)"), in_=acc[:], func=COPY)
             nc.sync.dma_start(out=out_rows[:, :, cols], in_=staged[:])
-            grouped = tile([P, PACK * CHUNK], BF16, "out_grouped%d" % c)
-            nc.vector.tensor_copy(out=grouped[:].rearrange("p (c i t) -> p c t i", i=4, t=PACK), in_=staged[:].rearrange("p t (c i) -> p c t i", i=4))
-            quantize(grouped[:], out_codes[:, cols], out_scales[:, cols])
-            if c >= 2:
-                both = slice(0 if c == 2 else cols.start, cols.stop)
-                nc.sync.dma_start(out=words_rows[:, both], in_=out_codes[:, both].bitcast(I32))
-        for q in range(4):
-            queue = nc.sync if q % 2 == 0 else nc.scalar
-            queue.dma_start(out=out_2[0, 4 * q : 4 * q + 4, :].bitcast(I32), in_=out_scales[32 * q : 32 * q + 4, :].bitcast(I32))
+            out_grouped = tile([P, PACK * CHUNK], BF16, "out_grouped%d" % c)
+            group(out_grouped, staged)
+            quantize(out_grouped[:], out_codes[:, cols], out_scales[:, cols])
+            if cols.stop in word_stores:
+                done = word_stores[cols.stop]
+                nc.sync.dma_start(out=words_rows[:, done], in_=out_codes[:, done].bitcast(I32))
+        for q, queue in enumerate([nc.sync, nc.scalar, nc.sync, nc.scalar]):
+            queue.dma_start(out=out_2[0, 4 * q : 4 * q + 4, :].bitcast(I32), in_=out_scales[live(q), :].bitcast(I32))

from contextlib import ExitStack

import concourse.mybir as mybir

K, T, S, V, N, H = 512, 2048, 512, 256, 512, 512
FLOPS = 2 * K * H * S + 2 * H * H * V + 2 * H * N * S

F32 = mybir.dt.float32
BF16 = mybir.dt.bfloat16
I32 = mybir.dt.int32
U32 = mybir.dt.uint32
U16 = mybir.dt.uint16
U8 = mybir.dt.uint8
FP8X4 = mybir.dt.float8_e4m3fn_x4
COPY = mybir.ActivationFunctionType.Copy
RELU = mybir.ActivationFunctionType.Relu
ADD = mybir.AluOpType.add

P = 128
PACK = 4
QUADRANTS = 4
BANK = 512
HALF = S // 2
CHUNK = BANK // PACK
W1_SCALAR = P // 2
W3_BYTES = 4 * N
LAST = PACK - 1
FIRST = LAST - 1


def tile_picked_prunefill_relu_po_kernel(tc, x_words, x_scales, w1, w2, w3_words, w3_scales, offs, la, lb, out_0, out_1, out_2):
    nc = tc.nc
    with ExitStack() as ctx:
        lists = ctx.enter_context(tc.tile_pool(name="lists", bufs=1))
        sb = ctx.enter_context(tc.tile_pool(name="sb", bufs=1))
        table = ctx.enter_context(tc.tile_pool(name="table", bufs=1))
        staging = ctx.enter_context(tc.tile_pool(name="staging", bufs=1))
        early = ctx.enter_context(tc.tile_pool(name="early", bufs=1))
        psum = ctx.enter_context(tc.psum_pool(name="psum", bufs=1))

        def tile(shape, dtype, name, tag=None):
            return sb.tile(shape, dtype, name=name, tag=tag or name, align_bytes=64)

        def placed(pool, offset, shape, dtype, name):
            return pool.tile(shape, dtype, name=name, align_bytes=64, offset=offset)

        def bank(b, name):
            return psum.tile([P, BANK], F32, name=name, tag="bank%d" % b)

        def live(q):
            return slice(32 * q, 32 * q + 4)

        def load_scale_rows(queues, plane, rows):
            for q, queue in enumerate(queues):
                queue.dma_start(out=plane[live(q), :].bitcast(I32), in_=rows[4 * q : 4 * q + 4, :].bitcast(I32))

        def load_weight(w, name, offset):
            raw = placed(staging, offset, [P, PACK, H], F32, name)
            nc.sync.dma_start(out=raw[:], in_=w.rearrange("(p j) c -> p j c", j=PACK))
            return raw

        def dealt_views(grouped, raw, ms):
            dst = grouped[:].rearrange("p (t m j) -> p m j t", t=PACK, j=PACK)[:, ms]
            src = raw[:].rearrange("p j (m t) -> p m j t", t=PACK)[:, ms]
            return dst, src

        def group(grouped, row_sets):
            nc.vector.tensor_copy(
                out=grouped[:].rearrange("p (c i t) -> p c t i", i=4, t=PACK),
                in_=row_sets[:].rearrange("p t (c i) -> p c t i", i=4),
            )

        def quantize(grouped, codes, scales):
            nc.vector.quantize_mx(out=codes.bitcast(FP8X4), scales=scales, in_=grouped)

        def product(out, w_codes, w_scales, t, codes, scales):
            cols = slice(P * t, P * (t + 1))
            nc.tensor.matmul_mx(
                out=out, lhsT=w_codes[:, cols].bitcast(FP8X4), lhsT_scale=w_scales[:, cols],
                rhs=codes.bitcast(FP8X4), rhs_scale=scales, start=True, stop=True,
            )

        offs_sb = lists.tile([P, S // 16], U16, name="offs_sb")
        la_sb = lists.tile([P, V // 16], U16, name="la_sb")
        lb_sb = lists.tile([P, V // 16], U16, name="lb_sb")

        x_plane = placed(early, 0, [P, T], U8, "x_plane")
        x_rows = tile([P, T], U8, "x_rows")
        w3_plane = tile([P, N], U8, "w3_plane")
        nc.vector.memset(x_plane[:].bitcast(I32), 0)
        nc.gpsimd.memset(w3_plane[:].bitcast(I32), 0)

        load_scale_rows([nc.sync, nc.scalar, nc.sync, nc.scalar], x_rows, x_scales[0])
        nc.sync.dma_start(offs_sb[:], offs)
        w1_raw = load_weight(w1, "w1_raw", 0)
        x_table = placed(table, 0, [P, T], I32, "x_table")
        nc.sync.dma_start(out=x_table[:], in_=x_words[0].rearrange("p n t -> p (n t)").bitcast(I32))
        nc.sync.dma_start(la_sb[:], la)
        nc.sync.dma_start(lb_sb[:], lb)
        load_scale_rows([nc.gpsimd, nc.sync, nc.gpsimd, nc.sync], w3_plane, w3_scales[0])

        for q in range(QUADRANTS):
            nc.vector.tensor_copy(out=x_plane[live(q), :].bitcast(I32), in_=x_rows[live(q), :].bitcast(I32))
        xg_scales = tile([P, S], U8, "xg_scales")
        nc.vector.tensor_copy(out=xg_scales[:], in_=x_plane[:].indirect(offs_sb[:]))

        w1_grouped = placed(early, T, [P, PACK * H], BF16, "w1_grouped")
        dst, src = dealt_views(w1_grouped, w1_raw, slice(0, W1_SCALAR))
        nc.scalar.activation(out=dst, in_=src, func=COPY)
        dst, src = dealt_views(w1_grouped, w1_raw, slice(W1_SCALAR, P))
        nc.vector.tensor_copy(out=dst, in_=src)
        w1_codes = tile([P, H], U32, "w1_codes")
        w1_scales = tile([P, H], U8, "w1_scales")
        quantize(w1_grouped[:], w1_codes[:], w1_scales[:])

        w3_table = placed(staging, 0, [P, N], I32, "w3_table")
        nc.sync.dma_start(out=w3_table[:], in_=w3_words[0].rearrange("p n t -> p (n t)").bitcast(I32))
        w2_raw = load_weight(w2, "w2_raw", W3_BYTES)

        xg_codes = placed(early, T // 2, [P, S], U32, "xg_codes")
        halves = [slice(0, HALF), slice(HALF, S)]
        for cols in halves:
            entries = offs_sb[:, cols.start // 16 : cols.stop // 16]
            nc.vector.tensor_copy(out=xg_codes[:, cols], in_=x_table[:].bitcast(U32).indirect(entries))

        y = [tile([P, S], F32, "y%d" % t) for t in range(PACK)]
        steps = [(t, cols) for cols in halves for t in range(2)] + [(t, slice(0, S)) for t in range(2, PACK)]
        for b, (t, cols) in enumerate(steps):
            acc = bank(b, "y_acc%d" % b)
            width = cols.stop - cols.start
            product(acc[:, :width], w1_codes, w1_scales, t, xg_codes[:, cols], xg_scales[:, cols])
            nc.scalar.activation(out=y[t][:, cols], in_=acc[:, :width], func=COPY)

        w3_codes = placed(table, 0, [P, N], I32, "w3_codes")
        w3_sc = placed(table, W3_BYTES, [P, N], U8, "w3_sc")
        nc.vector.tensor_copy(out=w3_sc[:].rearrange("p (t m) -> p t m", t=PACK), in_=w3_plane[:].rearrange("p (m t) -> p t m", t=PACK))
        nc.vector.tensor_copy(out=w3_codes[:].rearrange("p (t m) -> p m t", t=PACK), in_=w3_table[:].rearrange("p (m t) -> p m t", t=PACK))

        z_rows = placed(staging, 0, [P, PACK, V], BF16, "z_rows")
        for t in range(PACK):
            nc.vector.tensor_copy(out=z_rows[:, t, :], in_=y[t][:].indirect(la_sb[:]))
        z_grouped = tile([P, PACK * V], BF16, "z_grouped")
        group(z_grouped, z_rows)

        y_lb_first = placed(staging, 0, [P, 2, V], F32, "y_lb_first")
        y_lb = [y_lb_first[:, t, :] for t in range(2)]
        nc.vector.tensor_copy(out=y_lb[0], in_=y[0][:].indirect(lb_sb[:]))
        z_codes = tile([P, V], U32, "z_codes")
        z_scales = tile([P, V], U8, "z_scales")
        quantize(z_grouped[:], z_codes[:], z_scales[:])

        w2_grouped = placed(early, 0, [P, PACK * H], BF16, "w2_grouped")
        dst, src = dealt_views(w2_grouped, w2_raw, slice(0, P))
        nc.scalar.activation(out=dst, in_=src, func=COPY)
        w2_codes = tile([P, H], U32, "w2_codes")
        w2_scales = tile([P, H], U8, "w2_scales")
        nc.vector.tensor_copy(out=y_lb[1], in_=y[1][:].indirect(lb_sb[:]))
        quantize(w2_grouped[:], w2_codes[:], w2_scales[:])
        y_lb_last = placed(early, 0, [P, 2, V], F32, "y_lb_last")
        y_lb = y_lb + [y_lb_last[:, t, :] for t in range(2)]
        for t in range(2, PACK):
            nc.vector.tensor_copy(out=y_lb[t], in_=y[t][:].indirect(lb_sb[:]))

        order = [FIRST] + list(range(FIRST)) + [LAST]
        h = [tile([P, V], F32, "h%d" % t) for t in range(PACK)]
        loss = [tile([P, V], F32, "loss%d" % t) for t in range(LAST)]
        for t in order:
            acc = bank(t, "h_acc%d" % t)
            product(acc[:, :V], w2_codes, w2_scales, t, z_codes[:], z_scales[:])
            nc.scalar.activation(out=h[t][:], in_=acc[:, :V], func=RELU)
            if t != LAST:
                nc.scalar.activation(out=loss[t][:], in_=h[t][:], func=COPY, scale=-0.5)

        z2 = [tile([P, S], F32, "z2_%d" % t) for t in range(PACK)]
        z2_grouped = tile([P, S, PACK], BF16, "z2_grouped")
        for t in order:
            nc.vector.tensor_copy(out=z2[t][:].indirect(la_sb[:]), in_=h[t][:])
            nc.vector.tensor_tensor(out=z2[t][:].indirect(lb_sb[:]), in0=y_lb[t], in1=loss[t][:], op=ADD)
            if t != LAST:
                nc.scalar.activation(out=z2_grouped[:, :, t], in_=z2[t][:], func=COPY)
            if t == FIRST:
                loss.append(tile([P, V], F32, "loss%d" % LAST, "z2_%d" % FIRST))
                nc.scalar.activation(out=loss[LAST][:], in_=h[LAST][:], func=COPY, scale=-0.5)

        z2_codes = tile([P, S], U32, "z2_codes")
        z2_scales = tile([P, S], U8, "z2_scales")
        out_codes = tile([P, S], U32, "out_codes")
        out_scales = tile([P, S], U8, "out_scales")
        out_rows = out_0.rearrange("(p t) j -> p t j", t=PACK)
        words_rows = out_1[0].rearrange("p n t -> p (n t)").bitcast(I32)
        chunks = [slice(start, start + CHUNK) for start in range(0, S, CHUNK)]
        for c, cols in enumerate(chunks):
            if c % 2 == 0:
                nc.vector.tensor_copy(out=z2_grouped[:, cols, LAST], in_=z2[LAST][:, cols])
            else:
                nc.scalar.activation(out=z2_grouped[:, cols, LAST], in_=z2[LAST][:, cols], func=COPY)
        for cols in chunks:
            quantize(z2_grouped[:, cols, :].rearrange("p c t -> p (c t)"), z2_codes[:, cols], z2_scales[:, cols])

        word_stores = {S - CHUNK: slice(0, S - CHUNK), S: chunks[-1]}
        for c, cols in enumerate(chunks):
            acc = bank(PACK + c, "out_acc%d" % c)
            for t in range(PACK):
                product(acc[:, CHUNK * t : CHUNK * (t + 1)], w3_codes, w3_sc, t, z2_codes[:, cols], z2_scales[:, cols])
            staged = tile([P, PACK, CHUNK], F32, "staged%d" % c)
            nc.scalar.activation(out=staged[:].rearrange("p t c -> p (t c)"), in_=acc[:], func=COPY)
            nc.sync.dma_start(out=out_rows[:, :, cols], in_=staged[:])
            out_grouped = tile([P, PACK * CHUNK], BF16, "out_grouped%d" % c)
            group(out_grouped, staged)
            quantize(out_grouped[:], out_codes[:, cols], out_scales[:, cols])
            if cols.stop in word_stores:
                done = word_stores[cols.stop]
                nc.sync.dma_start(out=words_rows[:, done], in_=out_codes[:, done].bitcast(I32))
        for q, queue in enumerate([nc.sync, nc.scalar, nc.sync, nc.scalar]):
            queue.dma_start(out=out_2[0, 4 * q : 4 * q + 4, :].bitcast(I32), in_=out_scales[live(q), :].bitcast(I32))
